import numpy as np, ml_dtypes
CORES = [49,52,55,57,60,63,65,68,71,73,76,79]
N = 12
TK = 64
def setup_inputs(rng):
    return {"x": rng.standard_normal((N, 128, N * TK), dtype=np.float32).astype(ml_dtypes.bfloat16), "t": rng.standard_normal((N, 128, N * TK), dtype=np.float32).astype(ml_dtypes.bfloat16), "f1": (rng.standard_normal((N, 128, 128), dtype=np.float32) / 11).astype(ml_dtypes.bfloat16), "f2": (rng.standard_normal((N, 128, 128), dtype=np.float32) / 11).astype(ml_dtypes.bfloat16)}
def setup_inputs_big(rng):
    d = setup_inputs(rng)
    for k in ("x", "t", "f1", "f2"): d[k] = (d[k].astype(np.float32) * 1024.0).astype(d[k].dtype)
    return d
def setup_inputs_small(rng):
    d = setup_inputs(rng)
    for k in ("x", "t", "f1", "f2"): d[k] = (d[k].astype(np.float32) * (1 / 1024.0)).astype(d[k].dtype)
    return d
def reference(x, t, f1, f2):
    X, T, F1, F2 = x.astype(np.float64), t.astype(np.float64), f1.astype(np.float64), f2.astype(np.float64)
    y = np.zeros((N, 128, N * TK))
    for j in range(N):
        u = (F1[j].T @ X[j]) * T[j]
        for r in range(N):
            y[r][:, TK * j:TK * j + TK] = F2[r].T @ u[:, TK * r:TK * r + TK]
    return {"y": y.astype(ml_dtypes.bfloat16)}

@@ -1,0 +1,156 @@
+from concourse.bass import DstId, RemoteDMATransfer
+from concourse.mybir import AluOpType
+
+TK = 64
+NG = 4
+SCRATCH = {
+    "xs": ("sbuf", [128, 12 * TK], "bfloat16"),
+    "ts": ("sbuf", [128, 12 * TK], "bfloat16"),
+    "f1s": ("sbuf", [128, 128], "bfloat16"),
+    "f2s": ("sbuf", [128, 128], "bfloat16"),
+    "us": ("sbuf", [128, 12 * TK], "bfloat16"),
+    "land": ("sbuf", [128, 12 * TK], "bfloat16"),
+    "ys": ("sbuf", [128, 12 * TK], "bfloat16"),
+    "hubf": ("sbuf", [128, 3 * TK], "bfloat16"),
+    "hubm": ("sbuf", [128, 3 * TK], "bfloat16"),
+}
+for _i in range(NG):
+    SCRATCH["pa%d" % _i] = ("psum", [128, 512], "float32")
+    SCRATCH["pb%d" % _i] = ("psum", [128, 512], "float32")
+SEMAPHORES = (["ldf1", "ldf2", "vfar", "vmate", "vnear", "vown", "sent", "gchip", "gplane", "gmate", "gfar",
+               "hf", "hm"]
+              + [n + "%d" % i for n in ("lx", "lt", "ma", "mb", "cp", "st") for i in range(NG)])
+
+E_HUB_IN = 4
+E_HUB_OUT = 8
+E_PEER = 4
+
+
+def _plan(T, topo):
+    cores = list(T.cores)
+    chips = []
+    for c in cores:
+        if topo.chip(c) not in chips:
+            chips.append(topo.chip(c))
+    on = {a: [r for r, c in enumerate(cores) if topo.chip(c) == a] for a in chips}
+    kin, hubs = {}, {}
+    for a in chips:
+        mate = [b for b in chips if topo.mates(a, b)][0]
+        plane = [b for b in chips if topo.same_plane(a, b)][0]
+        far = [b for b in chips if b not in (a, mate, plane)][0]
+        kin[a] = (mate, plane, far)
+        there = [cores[r] for r in on[mate] + on[far]]
+        hubs[a] = [c for c in range(topo.CORES_PER_CHIP * topo.CHIPS)
+                   if topo.chip(c) == a and c not in cores and all(topo.may_write(c, d) for d in there)][:3]
+    return cores, on, kin, hubs
+
+
+def _take(topo, used, src, dst, n, top):
+    m = topo.mask(src, dst)
+    pool = [e for e in range(m.bit_length()) if (m >> e) & 1 and e not in used]
+    pick = pool[-n:] if top else pool[:n]
+    used.update(pick)
+    return sum(1 << e for e in pick)
+
+
+def _xfer(topo, dst, mask, sem, src_ap, dst_ap):
+    rid, pid, _ = topo.addr(dst)
+    return RemoteDMATransfer(dst_ids=[DstId(rid=rid, pnc=pid)], dma_engine_mask=mask, remote_sem=sem,
+                             src=src_ap, dst=dst_ap)
+
+
+def _cols(first, n=1):
+    return slice(TK * first, TK * (first + n))
+
+
+def _hub_program(g, core, T, topo, plan):
+    cores, on, kin, hubs = plan
+    a = topo.chip(core)
+    k = hubs[a].index(core)
+    mate, _, far = kin[a]
+    S = T.sem
+    for buf, full, b, sem in ((T.hubf, S.hf, far, S.gfar), (T.hubm, S.hm, mate, S.gmate)):
+        dst = cores[on[b][k]]
+        g.wait_ge(full, 3 * E_HUB_IN)
+        g.remote_dma_fused([_xfer(topo, dst, _take(topo, set(), core, dst, E_HUB_OUT, False), sem,
+                                  buf[:], T.land[:, _cols(on[a][0], 3)])], local_sem=S.sent)
+    g.wait_ge(S.sent, 2 * E_HUB_OUT)
+
+
+def rank_program(g, core, T, topo):
+    plan = _plan(T, topo)
+    cores, on, kin, hubs = plan
+    rank = T.rank_of(core)
+    if rank is None:
+        if topo.chip(core) in hubs and core in hubs[topo.chip(core)]:
+            _hub_program(g, core, T, topo, plan)
+        return
+    S = T.sem
+    a = topo.chip(core)
+    s = on[a].index(rank)
+    mate, plane, far = kin[a]
+    peers = [q for q in on[a] if q != rank]
+    first = (far, mate, plane, a)
+
+    g.scalar.dma_start(T.f1s[:], T.f1[:]).then_inc(S.ldf1, 16)
+    for i, b in enumerate(first):
+        c = _cols(on[b][0], 3)
+        q = g.sync if i % 2 == 0 else g.scalar
+        q.dma_start(T.xs[:, c], T.x[:, c]).then_inc(S["lx%d" % i], 16)
+        q.dma_start(T.ts[:, c], T.t[:, c]).then_inc(S["lt%d" % i], 16)
+    g.sync.dma_start(T.f2s[:], T.f2[:]).then_inc(S.ldf2, 16)
+
+    g.tensor.wait_ge(S.ldf1, 16)
+    for i, b in enumerate(first):
+        g.tensor.wait_ge(S["lx%d" % i], 16)
+        g.tensor.matmul(T["pa%d" % i][:, 0:3 * TK], T.f1s[:], T.xs[:, _cols(on[b][0], 3)],
+                        start=True, stop=True).then_inc(S["ma%d" % i], 1)
+        g.vector.wait_ge(S["lt%d" % i], 16)
+        g.vector.wait_ge(S["ma%d" % i], 1)
+        if b != a:
+            c = _cols(on[b][0], 3)
+            g.vector.tensor_tensor(T.us[:, c], T["pa%d" % i][:, 0:3 * TK], T.ts[:, c], AluOpType.mult).then_inc(
+                S.vfar if b == far else S.vmate if b == mate else S.vnear, 1)
+        else:
+            for k, q in enumerate(on[b]):
+                out, sem = (T.land, S.vown) if q == rank else (T.us, S.vnear)
+                g.vector.tensor_tensor(out[:, _cols(q)], T["pa%d" % i][:, _cols(k)], T.ts[:, _cols(q)],
+                                       AluOpType.mult).then_inc(sem, 1)
+
+    for ready, b, buf, sem in ((S.vfar, far, T.hubf, S.hf), (S.vmate, mate, T.hubm, S.hm)):
+        g.wait_ge(ready, 1)
+        used = set()
+        g.remote_dma_fused([_xfer(topo, h, _take(topo, used, core, h, E_HUB_IN, True), sem,
+                                  T.us[:, _cols(on[b][k])], buf[:, _cols(s)])
+                            for k, h in enumerate(hubs[a])], local_sem=S.sent)
+    g.wait_ge(S.vnear, 1 + len(peers))
+    used = set()
+    out = []
+    for k, q in sorted(enumerate(on[plane]), key=lambda kq: kq[0] != s):
+        out.append(_xfer(topo, cores[q], _take(topo, used, core, cores[q], 4 if k == s else 2, False), S.gplane,
+                         T.us[:, _cols(q)], T.land[:, _cols(rank)]))
+    for q in peers:
+        out.append(_xfer(topo, cores[q], _take(topo, used, core, cores[q], E_PEER, True), S.gchip,
+                         T.us[:, _cols(q)], T.land[:, _cols(rank)]))
+    g.remote_dma_fused(out, local_sem=S.sent)
+    g.wait_ge(S.sent, 2 * 3 * E_HUB_IN + 8 + 2 * E_PEER)
+
+    g.tensor.wait_ge(S.ldf2, 16)
+    for i, b in enumerate((a, plane, far, mate)):
+        c = _cols(on[b][0], 3)
+        pb = T["pb%d" % i]
+        if b == a:
+            g.tensor.wait_ge(S.vown, 1)
+            g.tensor.wait_ge(S.gchip, 2 * E_PEER)
+        elif b == plane:
+            g.tensor.wait_ge(S.gplane, 8)
+        else:
+            g.tensor.wait_ge(S.gmate if b == mate else S.gfar, E_HUB_OUT)
+        g.tensor.matmul(pb[:, 0:3 * TK], T.f2s[:], T.land[:, c], start=True, stop=True).then_inc(S["mb%d" % i], 1)
+        g.vector.wait_ge(S["mb%d" % i], 1)
+        g.vector.tensor_copy(T.ys[:, c], pb[:, 0:3 * TK]).then_inc(S["cp%d" % i], 1)
+        q = g.sync if i % 2 == 0 else g.scalar
+        q.wait_ge(S["cp%d" % i], 1)
+        q.dma_start(T.y[:, c], T.ys[:, c]).then_inc(S["st%d" % i], 16)
+    for i in range(NG):
+        (g.sync if i % 2 == 0 else g.scalar).wait_ge(S["st%d" % i], 16)

@@ -10,6 +10,7 @@ SCRATCH = {
     "f2s": ("sbuf", [128, 128], "bfloat16"),
     "us": ("sbuf", [128, 12 * TK], "bfloat16"),
     "land": ("sbuf", [128, 12 * TK], "bfloat16"),
+    "tl": ("sbuf", [128, 3 * TK], "bfloat16"),
     "ys": ("sbuf", [128, 12 * TK], "bfloat16"),
     "hubf": ("sbuf", [128, 3 * TK], "bfloat16"),
     "hubm": ("sbuf", [128, 3 * TK], "bfloat16"),
@@ -17,13 +18,14 @@ SCRATCH = {
 for _i in range(NG):
     SCRATCH["pa%d" % _i] = ("psum", [128, 512], "float32")
     SCRATCH["pb%d" % _i] = ("psum", [128, 512], "float32")
-SEMAPHORES = (["ldf1", "ldf2", "vfar", "vmate", "vnear", "vown", "sent", "gchip", "gplane", "gmate", "gfar",
-               "hf", "hm"]
+SEMAPHORES = (["ldf1", "ldf2", "vfar", "vmate", "vnear", "vown", "vpeer", "sent", "gt", "gchip", "gplane", "gmate",
+               "gfar", "hf", "hm"]
               + [n + "%d" % i for n in ("lx", "lt", "ma", "mb", "cp", "st") for i in range(NG)])
 
 E_HUB_IN = 4
 E_HUB_OUT = 8
 E_PEER = 4
+E_T = (8, 4)
 
 
 def _plan(T, topo):
@@ -91,32 +93,42 @@ def rank_program(g, core, T, topo):
     mate, plane, far = kin[a]
     peers = [q for q in on[a] if q != rank]
     first = (far, mate, plane, a)
+    own = first.index(a)
 
-    g.scalar.dma_start(T.f1s[:], T.f1[:]).then_inc(S.ldf1, 16)
-    for i, b in enumerate(first):
-        c = _cols(on[b][0], 3)
-        q = g.sync if i % 2 == 0 else g.scalar
-        q.dma_start(T.xs[:, c], T.x[:, c]).then_inc(S["lx%d" % i], 16)
-        q.dma_start(T.ts[:, c], T.t[:, c]).then_inc(S["lt%d" % i], 16)
-    g.sync.dma_start(T.f2s[:], T.f2[:]).then_inc(S.ldf2, 16)
+    def _grp(i):
+        return _cols(on[first[i]][0], 3)
+    loads = [(T.ts, T.t, _grp(own), S["lt%d" % own]), (T.f1s, T.f1, slice(None), S.ldf1)]
+    for i in range(NG):
+        loads.append((T.xs, T.x, _grp(i), S["lx%d" % i]))
+        if i != own:
+            loads.append((T.ts, T.t, _grp(i), S["lt%d" % i]))
+    loads.append((T.f2s, T.f2, slice(None), S.ldf2))
+    for n, (out, src, c, sem) in enumerate(loads):
+        (g.sync if n % 2 == 0 else g.scalar).dma_start(out[:, c], src[:, c]).then_inc(sem, 16)
 
     g.tensor.wait_ge(S.ldf1, 16)
     for i, b in enumerate(first):
+        pa = T["pa%d" % i]
         g.tensor.wait_ge(S["lx%d" % i], 16)
-        g.tensor.matmul(T["pa%d" % i][:, 0:3 * TK], T.f1s[:], T.xs[:, _cols(on[b][0], 3)],
-                        start=True, stop=True).then_inc(S["ma%d" % i], 1)
+        g.tensor.matmul(pa[:, 0:3 * TK], T.f1s[:], T.xs[:, _grp(i)], start=True, stop=True).then_inc(S["ma%d" % i], 1)
         g.vector.wait_ge(S["lt%d" % i], 16)
         g.vector.wait_ge(S["ma%d" % i], 1)
         if b != a:
-            c = _cols(on[b][0], 3)
-            g.vector.tensor_tensor(T.us[:, c], T["pa%d" % i][:, 0:3 * TK], T.ts[:, c], AluOpType.mult).then_inc(
+            c = _grp(i)
+            g.vector.tensor_tensor(T.us[:, c], pa[:, 0:3 * TK], T.ts[:, c], AluOpType.mult).then_inc(
                 S.vfar if b == far else S.vmate if b == mate else S.vnear, 1)
         else:
             for k, q in enumerate(on[b]):
-                out, sem = (T.land, S.vown) if q == rank else (T.us, S.vnear)
-                g.vector.tensor_tensor(out[:, _cols(q)], T["pa%d" % i][:, _cols(k)], T.ts[:, _cols(q)],
-                                       AluOpType.mult).then_inc(sem, 1)
+                if q == rank:
+                    g.vector.tensor_tensor(T.land[:, _cols(q)], pa[:, _cols(k)], T.ts[:, _cols(q)],
+                                           AluOpType.mult).then_inc(S.vown, 1)
+                else:
+                    g.vector.tensor_copy(T.us[:, _cols(q)], pa[:, _cols(k)]).then_inc(S.vnear, 1)
 
+    g.wait_ge(S["lt%d" % own], 16)
+    used = set()
+    g.remote_dma_fused([_xfer(topo, cores[q], _take(topo, used, core, cores[q], E_T[n], True), S.gt,
+                              T.ts[:, _cols(q)], T.tl[:, _cols(s)]) for n, q in enumerate(peers)], local_sem=S.sent)
     for ready, b, buf, sem in ((S.vfar, far, T.hubf, S.hf), (S.vmate, mate, T.hubm, S.hm)):
         g.wait_ge(ready, 1)
         used = set()
@@ -133,7 +145,13 @@ def rank_program(g, core, T, topo):
         out.append(_xfer(topo, cores[q], _take(topo, used, core, cores[q], E_PEER, True), S.gchip,
                          T.us[:, _cols(q)], T.land[:, _cols(rank)]))
     g.remote_dma_fused(out, local_sem=S.sent)
-    g.wait_ge(S.sent, 2 * 3 * E_HUB_IN + 8 + 2 * E_PEER)
+    g.wait_ge(S.sent, sum(E_T) + 2 * 3 * E_HUB_IN + 8 + 2 * E_PEER)
+
+    g.vector.wait_ge(S.gt, sum(E_T[[p for p in on[a] if p != q].index(rank)] for q in peers))
+    g.vector.wait_ge(S.gchip, 2 * E_PEER)
+    for q in peers:
+        g.vector.tensor_tensor(T.land[:, _cols(q)], T.land[:, _cols(q)], T.tl[:, _cols(on[a].index(q))],
+                               AluOpType.mult).then_inc(S.vpeer, 1)
 
     g.tensor.wait_ge(S.ldf2, 16)
     for i, b in enumerate((a, plane, far, mate)):
@@ -141,7 +159,7 @@ def rank_program(g, core, T, topo):
         pb = T["pb%d" % i]
         if b == a:
             g.tensor.wait_ge(S.vown, 1)
-            g.tensor.wait_ge(S.gchip, 2 * E_PEER)
+            g.tensor.wait_ge(S.vpeer, len(peers))
         elif b == plane:
             g.tensor.wait_ge(S.gplane, 8)
         else:

from concourse.bass import DstId, RemoteDMATransfer
from concourse.mybir import AluOpType

TK = 64
NG = 4
SCRATCH = {
    "xs": ("sbuf", [128, 12 * TK], "bfloat16"),
    "ts": ("sbuf", [128, 12 * TK], "bfloat16"),
    "f1s": ("sbuf", [128, 128], "bfloat16"),
    "f2s": ("sbuf", [128, 128], "bfloat16"),
    "us": ("sbuf", [128, 12 * TK], "bfloat16"),
    "land": ("sbuf", [128, 12 * TK], "bfloat16"),
    "tl": ("sbuf", [128, 3 * TK], "bfloat16"),
    "ys": ("sbuf", [128, 12 * TK], "bfloat16"),
    "hubf": ("sbuf", [128, 3 * TK], "bfloat16"),
    "hubm": ("sbuf", [128, 3 * TK], "bfloat16"),
}
for _i in range(NG):
    SCRATCH["pa%d" % _i] = ("psum", [128, 512], "float32")
    SCRATCH["pb%d" % _i] = ("psum", [128, 512], "float32")
SEMAPHORES = (["ldf1", "ldf2", "vfar", "vmate", "vnear", "vown", "vpeer", "sent", "gt", "gchip", "gplane", "gmate",
               "gfar", "hf", "hm"]
              + [n + "%d" % i for n in ("lx", "lt", "ma", "mb", "cp", "st") for i in range(NG)])

E_HUB_IN = 4
E_HUB_OUT = 8
E_PEER = 4
E_T = (8, 4)


def _plan(T, topo):
    cores = list(T.cores)
    chips = []
    for c in cores:
        if topo.chip(c) not in chips:
            chips.append(topo.chip(c))
    on = {a: [r for r, c in enumerate(cores) if topo.chip(c) == a] for a in chips}
    kin, hubs = {}, {}
    for a in chips:
        mate = [b for b in chips if topo.mates(a, b)][0]
        plane = [b for b in chips if topo.same_plane(a, b)][0]
        far = [b for b in chips if b not in (a, mate, plane)][0]
        kin[a] = (mate, plane, far)
        there = [cores[r] for r in on[mate] + on[far]]
        hubs[a] = [c for c in range(topo.CORES_PER_CHIP * topo.CHIPS)
                   if topo.chip(c) == a and c not in cores and all(topo.may_write(c, d) for d in there)][:3]
    return cores, on, kin, hubs


def _take(topo, used, src, dst, n, top):
    m = topo.mask(src, dst)
    pool = [e for e in range(m.bit_length()) if (m >> e) & 1 and e not in used]
    pick = pool[-n:] if top else pool[:n]
    used.update(pick)
    return sum(1 << e for e in pick)


def _xfer(topo, dst, mask, sem, src_ap, dst_ap):
    rid, pid, _ = topo.addr(dst)
    return RemoteDMATransfer(dst_ids=[DstId(rid=rid, pnc=pid)], dma_engine_mask=mask, remote_sem=sem,
                             src=src_ap, dst=dst_ap)


def _cols(first, n=1):
    return slice(TK * first, TK * (first + n))


def _hub_program(g, core, T, topo, plan):
    cores, on, kin, hubs = plan
    a = topo.chip(core)
    k = hubs[a].index(core)
    mate, _, far = kin[a]
    S = T.sem
    for buf, full, b, sem in ((T.hubf, S.hf, far, S.gfar), (T.hubm, S.hm, mate, S.gmate)):
        dst = cores[on[b][k]]
        g.wait_ge(full, 3 * E_HUB_IN)
        g.remote_dma_fused([_xfer(topo, dst, _take(topo, set(), core, dst, E_HUB_OUT, False), sem,
                                  buf[:], T.land[:, _cols(on[a][0], 3)])], local_sem=S.sent)
    g.wait_ge(S.sent, 2 * E_HUB_OUT)


def rank_program(g, core, T, topo):
    plan = _plan(T, topo)
    cores, on, kin, hubs = plan
    rank = T.rank_of(core)
    if rank is None:
        if topo.chip(core) in hubs and core in hubs[topo.chip(core)]:
            _hub_program(g, core, T, topo, plan)
        return
    S = T.sem
    a = topo.chip(core)
    s = on[a].index(rank)
    mate, plane, far = kin[a]
    peers = [q for q in on[a] if q != rank]
    first = (far, mate, plane, a)
    own = first.index(a)

    def _grp(i):
        return _cols(on[first[i]][0], 3)
    loads = [(T.ts, T.t, _grp(own), S["lt%d" % own]), (T.f1s, T.f1, slice(None), S.ldf1)]
    for i in range(NG):
        loads.append((T.xs, T.x, _grp(i), S["lx%d" % i]))
        if i != own:
            loads.append((T.ts, T.t, _grp(i), S["lt%d" % i]))
    loads.append((T.f2s, T.f2, slice(None), S.ldf2))
    for n, (out, src, c, sem) in enumerate(loads):
        (g.sync if n % 2 == 0 else g.scalar).dma_start(out[:, c], src[:, c]).then_inc(sem, 16)

    g.tensor.wait_ge(S.ldf1, 16)
    for i, b in enumerate(first):
        pa = T["pa%d" % i]
        g.tensor.wait_ge(S["lx%d" % i], 16)
        g.tensor.matmul(pa[:, 0:3 * TK], T.f1s[:], T.xs[:, _grp(i)], start=True, stop=True).then_inc(S["ma%d" % i], 1)
        g.vector.wait_ge(S["lt%d" % i], 16)
        g.vector.wait_ge(S["ma%d" % i], 1)
        if b != a:
            c = _grp(i)
            g.vector.tensor_tensor(T.us[:, c], pa[:, 0:3 * TK], T.ts[:, c], AluOpType.mult).then_inc(
                S.vfar if b == far else S.vmate if b == mate else S.vnear, 1)
        else:
            for k, q in enumerate(on[b]):
                if q == rank:
                    g.vector.tensor_tensor(T.land[:, _cols(q)], pa[:, _cols(k)], T.ts[:, _cols(q)],
                                           AluOpType.mult).then_inc(S.vown, 1)
                else:
                    g.vector.tensor_copy(T.us[:, _cols(q)], pa[:, _cols(k)]).then_inc(S.vnear, 1)

    g.wait_ge(S["lt%d" % own], 16)
    used = set()
    g.remote_dma_fused([_xfer(topo, cores[q], _take(topo, used, core, cores[q], E_T[n], True), S.gt,
                              T.ts[:, _cols(q)], T.tl[:, _cols(s)]) for n, q in enumerate(peers)], local_sem=S.sent)
    for ready, b, buf, sem in ((S.vfar, far, T.hubf, S.hf), (S.vmate, mate, T.hubm, S.hm)):
        g.wait_ge(ready, 1)
        used = set()
        g.remote_dma_fused([_xfer(topo, h, _take(topo, used, core, h, E_HUB_IN, True), sem,
                                  T.us[:, _cols(on[b][k])], buf[:, _cols(s)])
                            for k, h in enumerate(hubs[a])], local_sem=S.sent)
    g.wait_ge(S.vnear, 1 + len(peers))
    used = set()
    out = []
    for k, q in sorted(enumerate(on[plane]), key=lambda kq: kq[0] != s):
        out.append(_xfer(topo, cores[q], _take(topo, used, core, cores[q], 4 if k == s else 2, False), S.gplane,
                         T.us[:, _cols(q)], T.land[:, _cols(rank)]))
    for q in peers:
        out.append(_xfer(topo, cores[q], _take(topo, used, core, cores[q], E_PEER, True), S.gchip,
                         T.us[:, _cols(q)], T.land[:, _cols(rank)]))
    g.remote_dma_fused(out, local_sem=S.sent)
    g.wait_ge(S.sent, sum(E_T) + 2 * 3 * E_HUB_IN + 8 + 2 * E_PEER)

    g.vector.wait_ge(S.gt, sum(E_T[[p for p in on[a] if p != q].index(rank)] for q in peers))
    g.vector.wait_ge(S.gchip, 2 * E_PEER)
    for q in peers:
        g.vector.tensor_tensor(T.land[:, _cols(q)], T.land[:, _cols(q)], T.tl[:, _cols(on[a].index(q))],
                               AluOpType.mult).then_inc(S.vpeer, 1)

    g.tensor.wait_ge(S.ldf2, 16)
    for i, b in enumerate((a, plane, far, mate)):
        c = _cols(on[b][0], 3)
        pb = T["pb%d" % i]
        if b == a:
            g.tensor.wait_ge(S.vown, 1)
            g.tensor.wait_ge(S.vpeer, len(peers))
        elif b == plane:
            g.tensor.wait_ge(S.gplane, 8)
        else:
            g.tensor.wait_ge(S.gmate if b == mate else S.gfar, E_HUB_OUT)
        g.tensor.matmul(pb[:, 0:3 * TK], T.f2s[:], T.land[:, c], start=True, stop=True).then_inc(S["mb%d" % i], 1)
        g.vector.wait_ge(S["mb%d" % i], 1)
        g.vector.tensor_copy(T.ys[:, c], pb[:, 0:3 * TK]).then_inc(S["cp%d" % i], 1)
        q = g.sync if i % 2 == 0 else g.scalar
        q.wait_ge(S["cp%d" % i], 1)
        q.dma_start(T.y[:, c], T.ys[:, c]).then_inc(S["st%d" % i], 16)
    for i in range(NG):
        (g.sync if i % 2 == 0 else g.scalar).wait_ge(S["st%d" % i], 16)
